import numpy as np
import ml_dtypes


def mxq(x, axis, fmt="e4m3"):
    dtype, down = {"e4m3": (ml_dtypes.float8_e4m3fn, 7), "e5m2": (ml_dtypes.float8_e5m2, 14)}[fmt]
    v = np.moveaxis(np.asarray(x, np.float32).astype(ml_dtypes.bfloat16).astype(np.float64), axis, -1)
    blocks = v.reshape(v.shape[:-1] + (-1, 32))
    amax = np.abs(blocks).max(-1, keepdims=True)
    byte = np.maximum(np.where(amax > 0, np.frexp(amax)[1] - 1 + 127, 0) - down, 1)
    scale = np.exp2(byte - 127.0)
    codes = (blocks / scale).astype(np.float32).astype(dtype).astype(np.float64)
    return np.moveaxis((codes * scale).reshape(v.shape), -1, axis)


WIDE = False


def mx_kscale(k):
    if not WIDE:
        return np.ones(k)
    levels = np.array([10, -10, 5, -5, 0])
    if k % 512:
        return np.exp2(np.random.permutation(np.resize(levels, k // 32))).repeat(32)
    a = np.empty((k // 512, 16))
    for p in range(k // 512):
        a[p, :8] = np.random.permutation(np.resize(levels, 8))
        for g in range(8):
            far = levels[np.abs(levels - a[p, g]) >= 10]
            a[p, g + 8] = far[np.random.randint(len(far))]
    return np.exp2(a.ravel()).repeat(32)


def f64(x):
    return np.asarray(x).astype(np.float64)


def striped(idx):
    return np.tile(idx.reshape(-1, 16).T, (8, 1)).astype(np.uint16)


def unstriped(offs):
    return offs[:16].T.reshape(-1).astype(np.int64)


E2M1 = np.array([0.0, 0.5, 1.0, 1.5, 2.0, 3.0, 4.0, 6.0, -0.0, -0.5, -1.0, -1.5, -2.0, -3.0, -4.0, -6.0])


def pack_weight(w, fmt):
    k, n = w.shape
    w = f64(np.asarray(w, np.float32).astype(ml_dtypes.bfloat16)).reshape(k // 32, 32, n)
    amax = np.abs(w).max(1)
    if fmt == "e4m3":
        byte = np.frexp(amax)[1] - 1 + 127 - 7
    else:
        mant, ex = np.frexp(amax / 6.0)
        byte = np.where(mant > 0.5, ex, ex - 1) + 127
    byte = np.clip(np.where(amax > 0, byte, 1), 1, 254)
    scaled = (w * np.exp2(127.0 - byte)[:, None, :]).reshape(k, n).astype(np.float32)
    by_word = np.ascontiguousarray(scaled.reshape(k // 512, 128, 4, n).transpose(0, 1, 3, 2))
    if fmt == "e4m3":
        words = by_word.astype(ml_dtypes.float8_e4m3fn).view(np.uint8)
    else:
        c = by_word.astype(ml_dtypes.float4_e2m1fn).view(np.uint8) & 0xF
        words = (c[..., 0::2] | (c[..., 1::2] << 4)).reshape(k // 512, 128, 2 * n)
    return np.ascontiguousarray(words), np.ascontiguousarray(byte.astype(np.uint8).reshape(k // 512, 16, n))


def unpack_weight(words, scales, fmt):
    g, _, n = scales.shape
    words = np.ascontiguousarray(words).reshape(g, 128, n, -1)
    if fmt == "e4m3":
        vals = words.view(ml_dtypes.float8_e4m3fn).astype(np.float64)
    else:
        nib = np.empty((g, 128, n, 4), np.uint8)
        nib[..., 0::2] = words & 0xF
        nib[..., 1::2] = words >> 4
        vals = E2M1[nib]
    vals = vals * np.repeat(np.exp2(scales.astype(np.float64) - 127.0), 8, axis=1)[..., None]
    return vals.transpose(0, 1, 3, 2).reshape(g * 512, n)


def gelu(v):
    return 0.5 * v * (1.0 + np.tanh(np.sqrt(2.0 / np.pi) * (v + 0.044715 * v**3)))


K, T, S, P, H = 1024, 4096, 1024, 512, 1024

def setup_inputs():
    n = np.random.standard_normal
    s = mx_kscale(K)[:, None]
    u = mx_kscale(H)[:, None]
    tab_words, tab_scales = pack_weight(n((K, T)) * s, "e4m3")
    w4_words, w4_scales = pack_weight(2.2 * n((H, H)) / np.sqrt(H) / u, "e2m1")
    return {
        "tab_words": tab_words, "tab_scales": tab_scales,
        "offs": striped(np.random.permutation(T)[:S]),
        "pos1": striped(np.random.permutation(S)[:P]),
        "w1": (n((K, H)) / np.sqrt(K) / s).astype(np.float32),
        "sens": (1.3 * np.exp(0.3 * n(H))).astype(np.float32),
        "gain": (np.exp(0.3 * n(H)) * u[:, 0]).astype(np.float32),
        "tens": (0.8 * n((H, P))).astype(np.float32),
        "w4_words": w4_words, "w4_scales": w4_scales,
        "skip": (np.exp(0.3 * n(H)) / u[:, 0]).astype(np.float32),
        "wgo": np.exp(0.3 * n((128, P))).astype(np.float32),
    }

def reference(tab_words, tab_scales, offs, pos1, w1, sens, gain, tens, w4_words, w4_scales, skip, wgo):
    v = unpack_weight(tab_words, tab_scales, "e4m3")[:, unstriped(offs)]
    w1q = mxq(f64(w1), 0, "e4m3")
    reading = w1q.T @ v
    h = f64(gain)[:, None] * np.tanh(f64(sens)[:, None] * reading)
    tn = f64(tens)
    x = mxq(h[:, unstriped(pos1)] * tn, 0, "e4m3")
    w4 = unpack_weight(w4_words, w4_scales, "e2m1")
    y = np.tanh(w4.T @ x) + tn
    out = f64(skip)[:, None] * h
    out[:, unstriped(pos1)] = np.tile(f64(wgo), (H // 128, 1)) * y
    return out

from contextlib import ExitStack

import concourse.mybir as mybir
from concourse.masks import make_identity

K, T, S, NPICK, H = 1024, 4096, 1024, 512, 1024
FLOPS = 2 * K * H * S + 2 * H * H * NPICK

F32 = mybir.dt.float32
BF16 = mybir.dt.bfloat16
I32 = mybir.dt.int32
U32 = mybir.dt.uint32
U16 = mybir.dt.uint16
U8 = mybir.dt.uint8
FP8X4 = mybir.dt.float8_e4m3fn_x4
FP4X4 = mybir.dt.float4_e2m1fn_x4
MULT = mybir.AluOpType.mult
TANH = mybir.ActivationFunctionType.Tanh
COPY = mybir.ActivationFunctionType.Copy

P = 128
PACK = 4
KP = P * PACK
BANK = 512
HALF = NPICK // 2


def tile_list_towel_pile_gauge_kernel(
    tc, tab_words, tab_scales, offs, pos1, w1, sens, gain, tens, w4_words, w4_scales, skip, wgo, out
):
    nc = tc.nc
    with ExitStack() as ctx:
        keep = ctx.enter_context(tc.tile_pool(name="keep", bufs=1))
        ring = ctx.enter_context(tc.tile_pool(name="ring", bufs=4))
        reuse = ctx.enter_context(tc.tile_pool(name="reuse", bufs=1))
        psum = ctx.enter_context(tc.psum_pool(name="psum", bufs=1))

        def kept(shape, dtype, name):
            return keep.tile(shape, dtype, name=name, align_bytes=64)

        def placed(shape, dtype, name, kib):
            return reuse.tile(shape, dtype, name=name, align_bytes=64, offset=1024 * kib)

        offs_t = kept([P, S // 16], U16, "offs_t")
        pos_t = kept([P, NPICK // 16], U16, "pos_t")
        tab_w = [placed([P, T], I32, f"tab_w{a}", 16 * a) for a in range(2)]
        tab_s = placed([P, 2 * T], U8, "tab_s", 32)
        v_s = kept([P, 2 * S], U8, "v_s")
        nc.vector.memset(tab_s[:].bitcast(I32), 0)
        nc.vector.memset(v_s[:].bitcast(I32), 0)

        def load_tab(a, c0, c1):
            nc.sync.dma_start(tab_w[a][:, c0:c1], tab_words[a].rearrange("p t i -> p (t i)").bitcast(I32)[:, c0:c1])

        nc.sync.dma_start(offs_t[:], offs)
        nc.sync.dma_start(pos_t[:], pos1)
        vecs = {}
        for name, vec in (("sens", sens), ("gain", gain), ("skip", skip)):
            vecs[name] = kept([P, 2 * PACK], F32, name + "_t")
            nc.scalar.dma_start(
                vecs[name][:].rearrange("p (b t) -> p b t", b=2), vec.rearrange("(b p t) -> p b t", b=2, t=PACK)
            )
        for c in range(3):
            load_tab(0, 768 * c, 768 * (c + 1))
        nc.sync.dma_start(
            tab_s[0:P:8, :].bitcast(I32).rearrange("q (a c) -> q a c", a=2),
            tab_scales.rearrange("a q t -> q a t").bitcast(I32),
        )
        load_tab(0, 768 * 3, T)
        load_tab(1, 0, T)
        ident = kept([P, P], F32, "ident")
        make_identity(nc, ident[:])

        raw = {}

        def load_w1(a, b, kib):
            raw[a, b] = placed([P, PACK, KP], F32, f"raw{a}{b}", kib)
            nc.sync.dma_start(
                raw[a, b][:], w1[KP * a : KP * (a + 1), KP * b : KP * (b + 1)].rearrange("(p j) c -> p j c", j=PACK)
            )

        load_w1(0, 0, 40)
        load_w1(1, 0, 48)

        v_w = [kept([P, S], U32, f"v_w{a}") for a in range(2)]
        picked_s = kept([P, 2 * S], U8, "picked_s")
        for a in range(2):
            nc.vector.tensor_copy(picked_s[:, S * a : S * (a + 1)], tab_s[:, T * a : T * (a + 1)].indirect(offs_t[:]))
        for q in range(4):
            nc.scalar.dma_start(
                v_s[32 * q : 32 * q + 4, :].bitcast(I32), picked_s[32 * q : 32 * (q + 1) : 8, :].bitcast(I32)
            )
        for a in range(2):
            nc.vector.tensor_copy(v_w[a][:], tab_w[a][:].bitcast(U32).indirect(offs_t[:]))
        skip_gain = kept([P, 2 * PACK], F32, "skip_gain")
        nc.vector.tensor_tensor(skip_gain[:], vecs["skip"][:], vecs["gain"][:], MULT)

        load_w1(0, 1, 0)
        load_w1(1, 1, 8)
        tens_v = tens.rearrange("(b p u e) m -> b u p e m", b=2, u=2, e=2)
        tens_t = {}
        for b in range(2):
            for u in range(2):
                tens_t[b, u] = placed([P, 2, NPICK], F32, f"tens{b}{u}", 16 + 8 * b + 4 * u)
                nc.sync.dma_start(tens_t[b, u][:], tens_v[b, u])

        def tens_rows(b, t):
            return tens_t[b, t // 2][:, t % 2, :]

        w1_w, w1_s = {}, {}

        def round_w1(a, b, u, copy):
            grouped = ring.tile([P, 2 * KP], BF16, name=f"grp{a}{b}{u}", tag="grouped", align_bytes=64)
            copy(
                grouped[:].rearrange("p (e m j) -> p m j e", e=2, j=PACK),
                raw[a, b][:].rearrange("p j (m u e) -> p u m j e", u=2, e=2)[:, u],
            )
            return grouped

        def quantise_w1(a, b, u, grouped):
            w1_w[a, b, u] = kept([P, 2 * P], U32, f"w1_w{a}{b}{u}")
            w1_s[a, b, u] = kept([P, 2 * P], U8, f"w1_s{a}{b}{u}")
            nc.vector.quantize_mx(w1_w[a, b, u][:].bitcast(FP8X4), w1_s[a, b, u][:], grouped[:])

        def prepare_w1(a, b, first_copy, second_copy):
            first = round_w1(a, b, 0, first_copy)
            second = round_w1(a, b, 1, second_copy)
            quantise_w1(a, b, 0, first)
            quantise_w1(a, b, 1, second)

        th = {}

        def stage1(b, t):
            th[b, t] = kept([P, S], F32, f"th{b}{t}")
            cols = slice(P * (t % 2), P * (t % 2 + 1))
            for c in range(S // BANK):
                js = slice(BANK * c, BANK * (c + 1))
                acc = psum.tile([P, BANK], F32, name=f"acc{b}{t}{c}", tag="acc", bufs=5)
                for a in range(2):
                    nc.tensor.matmul_mx(
                        acc[:],
                        lhsT=w1_w[a, b, t // 2][:, cols].bitcast(FP8X4),
                        lhsT_scale=w1_s[a, b, t // 2][:, cols],
                        rhs=v_w[a][:, js].bitcast(FP8X4),
                        rhs_scale=v_s[:, S * a + BANK * c : S * a + BANK * (c + 1)],
                        start=(a == 0),
                        stop=(a == 1),
                    )
                nc.scalar.activation(th[b, t][:, js], acc[:], TANH, scale=vecs["sens"][:, 4 * b + t : 4 * b + t + 1])

        gt = {}

        def gain_tens(b, t):
            gt[b, t] = kept([P, NPICK], F32, f"gt{b}{t}")
            nc.scalar.activation(gt[b, t][:], tens_rows(b, t), COPY, scale=vecs["gain"][:, 4 * b + t : 4 * b + t + 1])

        def pick(b, t, xs, m0, n):
            nc.vector.tensor_tensor(
                xs[:, t, :],
                th[b, t][:].indirect(pos_t[:, m0 // 16 : (m0 + n) // 16]),
                gt[b, t][:, m0 : m0 + n],
                MULT,
            )

        def quantise_x(xs, n, name):
            xb = kept([P, PACK * n], BF16, "xb" + name)
            nc.vector.tensor_copy(
                xb[:].rearrange("p (c i t) -> p c t i", i=4, t=PACK), xs[:].rearrange("p t (c i) -> p c t i", i=4)
            )
            x_w = kept([P, n], U32, "x_w" + name)
            x_s = kept([P, n], U8, "x_s" + name)
            nc.vector.quantize_mx(x_w[:].bitcast(FP8X4), x_s[:], xb[:])
            return x_w, x_s

        prepare_w1(0, 0, nc.scalar.copy, nc.scalar.copy)
        prepare_w1(1, 0, nc.vector.tensor_copy, nc.scalar.copy)

        w4_w = placed([P, 2 * 2 * H], U8, "w4_w", 40)
        w4_s = placed([P, 2 * H], U8, "w4_s", 44)
        nc.gpsimd.memset(w4_s[:].bitcast(I32), 0)
        nc.sync.dma_start(
            w4_w[:].bitcast(I32).rearrange("p (a c) -> p a c", a=2), w4_words.rearrange("a p c -> p a c").bitcast(I32)
        )
        for q in range(4):
            nc.sync.dma_start(
                w4_s[32 * q : 32 * q + 4, :].bitcast(I32).rearrange("p (a c) -> p a c", a=2),
                w4_scales[:, 4 * q : 4 * q + 4, :].rearrange("a r c -> r a c").bitcast(I32),
            )
        wgo_t = placed([P, PACK, NPICK], F32, "wgo_t", 48)
        for q in range(4):
            nc.sync.dma_start(wgo_t[32 * q : 32 * (q + 1), :, :], wgo.rearrange("(p t) m -> p t m", t=PACK))

        for t in range(3):
            stage1(0, t)
        prepare_w1(0, 1, nc.vector.tensor_copy, nc.vector.tensor_copy)
        prepare_w1(1, 1, nc.vector.tensor_copy, nc.vector.tensor_copy)
        gain_tens(0, 0)
        stage1(0, 3)
        xs0 = placed([P, PACK, NPICK], F32, "xs0", 32)
        for t in range(PACK):
            if t > 0:
                gain_tens(0, t)
            pick(0, t, xs0, 0, NPICK)
        x0 = quantise_x(xs0, NPICK, "0")
        xs1 = keep.tile([P, PACK, HALF], F32, name="xs1a", tag="xs1", align_bytes=64)
        for t in range(PACK):
            stage1(1, t)
            gain_tens(1, t)
            pick(1, t, xs1, 0, HALF)
        x1 = [quantise_x(xs1, HALF, "1a")]

        ty = {}

        def stage2(b, i):
            z = psum.tile([P, BANK], F32, name=f"z{b}{i}", tag="acc", bufs=5)
            operands = ((x0, P * i), (x1[i // 2], P * (i % 2)))
            for a in range(2):
                (x_w, x_s), m0 = operands[a]
                nc.tensor.matmul_mx(
                    z[:],
                    lhsT=x_w[:, m0 : m0 + P].bitcast(FP8X4),
                    lhsT_scale=x_s[:, m0 : m0 + P],
                    rhs=w4_w[:, 2 * (H * a + KP * b) : 2 * (H * a + KP * (b + 1))].bitcast(FP4X4),
                    rhs_scale=w4_s[:, H * a + KP * b : H * a + KP * (b + 1)],
                    start=(a == 0),
                    stop=(a == 1),
                )
            ty[b, i] = kept([P, KP], F32, f"ty{b}{i}")
            nc.scalar.activation(
                ty[b, i][:].rearrange("p (t q) -> p t q", t=PACK), z[:].rearrange("p (q t) -> p t q", t=PACK), TANH
            )

        page, tens_tr = {}, {}

        def open_page(b, t):
            page[b, t] = ring.tile([P, S], F32, name=f"page{b}{t}", tag="page", align_bytes=64)
            nc.scalar.activation(page[b, t][:], th[b, t][:], COPY, scale=skip_gain[:, 4 * b + t : 4 * b + t + 1])
            turned = psum.tile([P, BANK], F32, name=f"turned{b}{t}", tag="turned", bufs=1)
            for i in range(4):
                nc.tensor.transpose(turned[:, P * i : P * (i + 1)], tens_rows(b, t)[:, P * i : P * (i + 1)], ident[:])
            tens_tr[b, t] = ring.tile([P, NPICK], F32, name=f"tens_tr{b}{t}", tag="tens_tr", bufs=3, align_bytes=64)
            nc.scalar.copy(tens_tr[b, t][:], turned[:])

        def put(b, t, m0, n):
            ysum = psum.tile([P, n], F32, name=f"ysum{b}{t}{m0}", tag="ysum", bufs=2)
            for i in range(m0 // P, (m0 + n) // P):
                dst = ysum[:, P * i - m0 : P * (i + 1) - m0]
                nc.tensor.matmul(
                    dst, tens_tr[b, t][:, P * i : P * (i + 1)], ident[:], start=True, stop=False, is_transpose=True
                )
                nc.tensor.matmul(
                    dst, ty[b, i][:, P * t : P * (t + 1)], ident[:], start=False, stop=True, is_transpose=True
                )
            y = ring.tile([P, n], F32, name=f"y{b}{t}{m0}", tag="y", bufs=3, align_bytes=64)
            nc.scalar.copy(y[:], ysum[:])
            nc.vector.tensor_tensor(
                page[b, t][:].indirect(pos_t[:, m0 // 16 : (m0 + n) // 16]), y[:], wgo_t[:, t, m0 : m0 + n], MULT
            )

        out_v = out.rearrange("(b p t) j -> b t p j", b=2, t=PACK)

        def store(b, t):
            nc.sync.dma_start(out_v[b, t], page[b, t][:])

        open_page(0, 0)
        stage2(0, 0)
        stage2(0, 1)
        xs1 = keep.tile([P, PACK, HALF], F32, name="xs1b", tag="xs1", align_bytes=64)
        for t in range(PACK):
            pick(1, t, xs1, HALF, HALF)
        x1.append(quantise_x(xs1, HALF, "1b"))
        put(0, 0, 0, HALF)
        open_page(0, 1)
        put(0, 1, 0, HALF)
        stage2(0, 2)
        stage2(0, 3)
        for t in range(2):
            put(0, t, HALF, HALF)
            store(0, t)
        for t in range(2, PACK):
            open_page(0, t)
            put(0, t, 0, NPICK)
            store(0, t)
            stage2(1, 2 * (t - 2))
            stage2(1, 2 * (t - 2) + 1)
        for t in range(PACK):
            open_page(1, t)
            put(1, t, 0, NPICK)
            store(1, t)
